import numpy as np
import ml_dtypes


def mxq(x, axis, fmt="e4m3"):
    dtype, down = {"e4m3": (ml_dtypes.float8_e4m3fn, 7), "e5m2": (ml_dtypes.float8_e5m2, 14)}[fmt]
    v = np.moveaxis(np.asarray(x, np.float32).astype(ml_dtypes.bfloat16).astype(np.float64), axis, -1)
    blocks = v.reshape(v.shape[:-1] + (-1, 32))
    amax = np.abs(blocks).max(-1, keepdims=True)
    byte = np.maximum(np.where(amax > 0, np.frexp(amax)[1] - 1 + 127, 0) - down, 1)
    scale = np.exp2(byte - 127.0)
    codes = (blocks / scale).astype(np.float32).astype(dtype).astype(np.float64)
    return np.moveaxis((codes * scale).reshape(v.shape), -1, axis)


WIDE = False


def mx_kscale(k):
    if not WIDE:
        return np.ones(k)
    levels = np.array([10, -10, 5, -5, 0])
    if k % 512:
        return np.exp2(np.random.permutation(np.resize(levels, k // 32))).repeat(32)
    a = np.empty((k // 512, 16))
    for p in range(k // 512):
        a[p, :8] = np.random.permutation(np.resize(levels, 8))
        for g in range(8):
            far = levels[np.abs(levels - a[p, g]) >= 10]
            a[p, g + 8] = far[np.random.randint(len(far))]
    return np.exp2(a.ravel()).repeat(32)


def f64(x):
    return np.asarray(x).astype(np.float64)


def striped(idx):
    return np.tile(np.asarray(idx).reshape(-1, 16).T, (8, 1)).astype(np.uint16)


def unstriped(offs):
    return offs[:16].T.reshape(-1).astype(np.int64)


E2M1 = np.array([0.0, 0.5, 1.0, 1.5, 2.0, 3.0, 4.0, 6.0, -0.0, -0.5, -1.0, -1.5, -2.0, -3.0, -4.0, -6.0])


def pack_weight(w, fmt):
    k, n = w.shape
    w = f64(np.asarray(w, np.float32).astype(ml_dtypes.bfloat16)).reshape(k // 32, 32, n)
    amax = np.abs(w).max(1)
    if fmt == "e4m3":
        byte = np.frexp(amax)[1] - 1 + 127 - 7
    else:
        mant, ex = np.frexp(amax / 6.0)
        byte = np.where(mant > 0.5, ex, ex - 1) + 127
    byte = np.clip(np.where(amax > 0, byte, 1), 1, 254)
    scaled = (w * np.exp2(127.0 - byte)[:, None, :]).reshape(k, n).astype(np.float32)
    by_word = np.ascontiguousarray(scaled.reshape(k // 512, 128, 4, n).transpose(0, 1, 3, 2))
    if fmt == "e4m3":
        words = by_word.astype(ml_dtypes.float8_e4m3fn).view(np.uint8)
    else:
        c = by_word.astype(ml_dtypes.float4_e2m1fn).view(np.uint8) & 0xF
        words = (c[..., 0::2] | (c[..., 1::2] << 4)).reshape(k // 512, 128, 2 * n)
    return np.ascontiguousarray(words), np.ascontiguousarray(byte.astype(np.uint8).reshape(k // 512, 16, n))


def unpack_weight(words, scales, fmt):
    g, _, n = scales.shape
    words = np.ascontiguousarray(words).reshape(g, 128, n, -1)
    if fmt == "e4m3":
        vals = words.view(ml_dtypes.float8_e4m3fn).astype(np.float64)
    else:
        nib = np.empty((g, 128, n, 4), np.uint8)
        nib[..., 0::2] = words & 0xF
        nib[..., 1::2] = words >> 4
        vals = E2M1[nib]
    vals = vals * np.repeat(np.exp2(scales.astype(np.float64) - 127.0), 8, axis=1)[..., None]
    return vals.transpose(0, 1, 3, 2).reshape(g * 512, n)


def sigmoid(v):
    return 1.0 / (1.0 + np.exp(-v))


D, T, I, Q, E = 512, 2048, 512, 128, 512


def setup_inputs():
    n = np.random.standard_normal
    idx = np.random.permutation(T)[:I]
    idx2 = np.random.permutation(T)[:I]
    idx3 = np.random.permutation(T)[:I]
    fd = mx_kscale(D)
    fi = mx_kscale(I)
    ti = np.ones(T)
    ti[idx] = fi
    keysp = pack_weight(n((D, T)) / fd[:, None], "e4m3")
    return {
        "query": (n((D, Q)) * 0.9 / np.sqrt(D) * fd[:, None]).astype(np.float32),
        "keys_words": keysp[0],
        "keys_scales": keysp[1],
        "lam": (np.random.uniform(0.3, 0.9, (Q, 1))).astype(np.float32),
        "damp": (np.random.uniform(1.0, 4.0, (Q, 1))).astype(np.float32),
        "os": (np.random.uniform(4.0, 16.0, (1, I)) * fi).astype(np.float32),
        "vals": (n((E, T)) / ti).astype(np.float32),
        "before": (n((Q, E)) * 1.0).astype(np.float32),
        "eager2": (np.random.uniform(0.5, 1.5, (Q, 1))).astype(np.float32),
        "offs": striped(idx),
        "offs2": striped(idx2),
        "offs3": striped(idx3),
    }


def reference(query, keys_words, keys_scales, lam, damp, os, vals, before, eager2, offs, offs2, offs3):
    idx = unstriped(offs)
    idx2 = unstriped(offs2)
    idx3 = unstriped(offs3)
    keysu = unpack_weight(keys_words, keys_scales, "e4m3")
    queryq = mxq(f64(query), 0, "e4m3")
    a = queryq.T @ keysu
    s = a[:, idx] + np.maximum(a[:, idx2], a[:, idx3]) * f64(lam)
    p = np.exp(s - np.max(s, axis=1, keepdims=True))
    r = p / np.sum(p, axis=1, keepdims=True) * 512.0
    u0 = np.log(r * f64(damp) + 1.0)
    w = u0 / np.sum(u0, axis=1, keepdims=True)
    wo1 = w * f64(os)
    wt1 = wo1.T
    vt1 = f64(vals)[:, idx].T
    wt1q = mxq(wt1, 0, "e4m3")
    vt1q = mxq(vt1, 0, "e4m3")
    o = wt1q.T @ vt1q
    df0 = o - f64(before)
    gt1 = sigmoid(np.mean(np.square(df0), axis=1, keepdims=True) * f64(eager2) - 1.0)
    y = f64(before) + df0 * gt1
    return y

@@ -1,0 +1,229 @@
+from contextlib import ExitStack
+
+import concourse.mybir as mybir
+from concourse.masks import make_identity
+
+D, T, I, Q, E = 512, 2048, 512, 128, 512
+FLOPS = 2 * D * Q * T + 2 * I * Q * E
+
+F32 = mybir.dt.float32
+BF16 = mybir.dt.bfloat16
+I32 = mybir.dt.int32
+U32 = mybir.dt.uint32
+U16 = mybir.dt.uint16
+U8 = mybir.dt.uint8
+FP8X4 = mybir.dt.float8_e4m3fn_x4
+ALU = mybir.AluOpType
+ACT = mybir.ActivationFunctionType
+AXIS = mybir.AxisListType
+
+P = 128
+PACK = 4
+BANK = 512
+CHUNKS = T // BANK
+BLOCKS = E // P
+
+
+def tile_attend_lookahead_dampened_movedbychange_kernel(
+    tc, query, keys_words, keys_scales, lam, damp, slot_factor, vals, before, eager2, offs, offs2, offs3, out
+):
+    nc = tc.nc
+    with ExitStack() as ctx:
+        sb = ctx.enter_context(tc.tile_pool(name="sb", bufs=1))
+        acc = ctx.enter_context(tc.psum_pool(name="acc", bufs=4))
+        turn = ctx.enter_context(tc.psum_pool(name="turn", bufs=4))
+
+        k_scales = sb.tile([P, BANK], U8, align_bytes=64)
+        nc.vector.memset(k_scales[:].bitcast(I32), 0)
+        for quad in range(4):
+            nc.sync.dma_start(
+                out=k_scales[32 * quad : 32 * quad + 16, :].bitcast(I32),
+                in_=keys_scales[0, 4 * quad : 4 * quad + 4, :].rearrange("r (c n) -> c r n", c=CHUNKS).bitcast(I32),
+            )
+        q_raw = sb.tile([P, PACK, Q], F32)
+        nc.sync.dma_start(out=q_raw[:], in_=query.rearrange("(p j) q -> p j q", j=PACK))
+        key_bytes = keys_words[0].rearrange("p n t -> p (n t)")
+        k_codes = []
+        for c in range(CHUNKS):
+            codes = sb.tile([P, BANK], U32, name="k_codes%d" % c, align_bytes=64)
+            nc.sync.dma_start(
+                out=codes[:].bitcast(I32), in_=key_bytes[:, c * BANK * PACK : (c + 1) * BANK * PACK].bitcast(I32)
+            )
+            k_codes.append(codes)
+        list2 = sb.tile([P, I // 16], U16)
+        nc.sync.dma_start(list2[:], offs2)
+        list3 = sb.tile([P, I // 16], U16)
+        nc.sync.dma_start(list3[:], offs3)
+        list1 = sb.tile([P, I // 16], U16)
+        nc.sync.dma_start(list1[:], offs)
+        os_col = sb.tile([P, PACK], F32)
+        lam_sb = sb.tile([P, 1], F32)
+        damp_sb = sb.tile([P, 1], F32)
+        eager_sb = sb.tile([P, 1], F32)
+        small_after = (
+            ((lam_sb, lam),),
+            ((damp_sb, damp), (os_col, slot_factor.rearrange("o (p t) -> p (o t)", t=PACK))),
+            ((eager_sb, eager2),),
+            (),
+        )
+        v_pool = []
+        for b in range(BLOCKS):
+            pool_rows = sb.tile([P, T], F32, name="v_pool%d" % b)
+            nc.sync.dma_start(out=pool_rows[:], in_=vals[b * P : (b + 1) * P, :])
+            v_pool.append(pool_rows)
+            for small, source in small_after[b]:
+                nc.sync.dma_start(out=small[:], in_=source)
+        before_sb = sb.tile([P, E], F32)
+        nc.sync.dma_start(out=before_sb[:], in_=before)
+
+        ident = sb.tile([P, P], F32)
+        make_identity(nc, ident[:])
+
+        q_bf = sb.tile([P, Q, PACK], BF16, align_bytes=64)
+        nc.vector.tensor_copy(out=q_bf[:], in_=q_raw[:].rearrange("p j q -> p q j"))
+        q_codes = sb.tile([P, Q], U32, align_bytes=64)
+        q_scales = sb.tile([P, Q], U8, align_bytes=64)
+        nc.vector.quantize_mx(
+            out=q_codes[:].bitcast(FP8X4), scales=q_scales[:], in_=q_bf[:].rearrange("p q j -> p (q j)")
+        )
+
+        a_sb = sb.tile([P, T], F32)
+        for c in range(CHUNKS):
+            a_ps = acc.tile([P, BANK], F32, tag="acc", name="a_ps")
+            nc.tensor.matmul_mx(
+                out=a_ps[:],
+                lhsT=q_codes[:].bitcast(FP8X4),
+                lhsT_scale=q_scales[:],
+                rhs=k_codes[c][:].bitcast(FP8X4),
+                rhs_scale=k_scales[4 * c : P, :],
+                start=True,
+                stop=True,
+            )
+            cols = slice(c * BANK, (c + 1) * BANK)
+            if c % 2 == 0:
+                nc.vector.tensor_copy(out=a_sb[:, cols], in_=a_ps[:])
+            else:
+                nc.scalar.copy(out=a_sb[:, cols], in_=a_ps[:])
+
+        a2 = sb.tile([P, I], F32)
+        nc.scalar.activation(a2[:], a_sb[:].indirect(list2[:]), ACT.Copy)
+        a3 = sb.tile([P, I], F32)
+        nc.vector.tensor_copy(a3[:], a_sb[:].indirect(list3[:]))
+        a1 = sb.tile([P, I], F32)
+        nc.scalar.activation(a1[:], a_sb[:].indirect(list1[:]), ACT.Copy)
+        follower = sb.tile([P, I], F32)
+        nc.vector.tensor_tensor(out=follower[:], in0=a2[:], in1=a3[:], op=ALU.max)
+        score = sb.tile([P, I], F32)
+        nc.vector.scalar_tensor_tensor(
+            out=score[:], in0=follower[:], scalar=lam_sb[:], in1=a1[:], op0=ALU.mult, op1=ALU.add
+        )
+        neg_max = sb.tile([P, 1], F32)
+        nc.vector.tensor_reduce(out=neg_max[:], in_=score[:], axis=AXIS.X, op=ALU.max, negate=True)
+        p_sb = sb.tile([P, I], F32)
+        p_sum = sb.tile([P, 1], F32)
+        nc.scalar.activation(out=p_sb[:], in_=score[:], func=ACT.Exp, bias=neg_max[:], accum_out=p_sum[:])
+        p_inv = sb.tile([P, 1], F32)
+        nc.vector.reciprocal(out=p_inv[:], in_=p_sum[:])
+        gain = sb.tile([P, 1], F32)
+        nc.vector.tensor_scalar(
+            out=gain[:], in0=p_inv[:], scalar1=damp_sb[:], scalar2=float(I), op0=ALU.mult, op1=ALU.mult
+        )
+        part = sb.tile([P, I], F32)
+        part_sum = sb.tile([P, 1], F32)
+        nc.scalar.activation(out=part[:], in_=p_sb[:], func=ACT.Ln, bias=1.0, scale=gain[:], accum_out=part_sum[:])
+        part_inv = sb.tile([P, 1], F32)
+        nc.vector.reciprocal(out=part_inv[:], in_=part_sum[:])
+
+        os_ps = turn.tile([P, PACK, P], F32, tag="turn", name="os_ps")
+        for t in range(PACK):
+            nc.tensor.transpose(os_ps[:, t, :], os_col[:, t : t + 1].to_broadcast([P, P]), ident[:])
+        os_rows = sb.tile([P, P, PACK], F32)
+        nc.scalar.copy(out=os_rows[:], in_=os_ps[:].rearrange("q t p -> q p t"))
+
+        w_bf = sb.tile([P, I], BF16)
+        nc.vector.scalar_tensor_tensor(
+            out=w_bf[:],
+            in0=part[:],
+            scalar=part_inv[:],
+            in1=os_rows[:].rearrange("q p t -> q (p t)"),
+            op0=ALU.mult,
+            op1=ALU.mult,
+        )
+
+        def turn_and_quantise(rows_bf, name, copy, codes, scales):
+            words = rows_bf[:].bitcast(F32)
+            turned = turn.tile([P, 2, P], F32, tag="turn", name="turned")
+            for u in range(2):
+                nc.tensor.transpose(turned[:, u, :], words[:, u : I // 2 : 2], ident[:])
+            grouped = sb.tile([P, P * PACK], BF16, name=name, align_bytes=64)
+            copy(
+                out=grouped[:].bitcast(F32).rearrange("p (r u) -> p r u", u=2),
+                in_=turned[:].rearrange("p u r -> p r u"),
+            )
+            nc.vector.quantize_mx(out=codes.bitcast(FP8X4), scales=scales, in_=grouped[:])
+
+        w_codes = sb.tile([P, Q], U32, align_bytes=64)
+        w_scales = sb.tile([P, Q], U8, align_bytes=64)
+        turn_and_quantise(w_bf, "w_grouped", nc.scalar.copy, w_codes[:], w_scales[:])
+
+        v_codes = sb.tile([P, E], U32, align_bytes=64)
+        v_scales = sb.tile([P, E], U8, align_bytes=64)
+        half = I // 2
+        for b in range(BLOCKS):
+            picked = sb.tile([P, I], BF16, name="picked%d" % b)
+            if b == 0:
+                nc.scalar.activation(picked[:], v_pool[b][:].indirect(list1[:]), ACT.Copy)
+            elif b < BLOCKS - 1:
+                nc.vector.tensor_copy(picked[:], v_pool[b][:].indirect(list1[:]))
+            else:
+                nc.vector.tensor_copy(picked[:, :half], v_pool[b][:].indirect(list1[:, : half // 16]))
+                nc.scalar.activation(picked[:, half:], v_pool[b][:].indirect(list1[:, half // 16 :]), ACT.Copy)
+            cols = slice(b * P, (b + 1) * P)
+            turn_and_quantise(picked, "v_grouped%d" % b, nc.vector.tensor_copy, v_codes[:, cols], v_scales[:, cols])
+
+        def second_product(o_out, cols):
+            nc.tensor.matmul_mx(
+                out=o_out,
+                lhsT=w_codes[:].bitcast(FP8X4),
+                lhsT_scale=w_scales[:],
+                rhs=v_codes[:, cols].bitcast(FP8X4),
+                rhs_scale=v_scales[:, cols],
+                start=True,
+                stop=True,
+            )
+
+        early = E - P
+        o_early = acc.tile([P, early], F32, tag="acc", name="o_early")
+        second_product(o_early[:, : 2 * P], slice(0, 2 * P))
+        second_product(o_early[:, 2 * P :], slice(2 * P, early))
+        o_late = acc.tile([P, P], F32, tag="acc", name="o_late")
+        second_product(o_late[:], slice(early, E))
+
+        eager_mean = sb.tile([P, 1], F32)
+        nc.vector.tensor_scalar(out=eager_mean[:], in0=eager_sb[:], scalar1=1.0 / E, scalar2=None, op0=ALU.mult)
+        change = sb.tile([P, E], F32)
+        squares = sb.tile([P, E], F32)
+        sum_early = sb.tile([P, 1], F32)
+        sum_late = sb.tile([P, 1], F32)
+        nc.vector.tensor_tensor(out=change[:, :early], in0=o_early[:], in1=before_sb[:, :early], op=ALU.subtract)
+        nc.scalar.activation(out=squares[:, :early], in_=change[:, :early], func=ACT.Square, accum_out=sum_early[:])
+        nc.vector.tensor_tensor(out=change[:, early:], in0=o_late[:], in1=before_sb[:, early:], op=ALU.subtract)
+        nc.scalar.activation(out=squares[:, early:], in_=change[:, early:], func=ACT.Square, accum_out=sum_late[:])
+        gate_bias = sb.tile([P, 1], F32)
+        nc.vector.tensor_scalar(
+            out=gate_bias[:], in0=sum_early[:], scalar1=eager_mean[:], scalar2=-1.0, op0=ALU.mult, op1=ALU.add
+        )
+        gate = sb.tile([P, 1], F32)
+        nc.scalar.activation(out=gate[:], in_=sum_late[:], func=ACT.Sigmoid, bias=gate_bias[:], scale=eager_mean[:])
+        result = sb.tile([P, E], F32)
+        for h, queue in enumerate((nc.sync, nc.scalar)):
+            cols = slice(h * E // 2, (h + 1) * E // 2)
+            nc.vector.scalar_tensor_tensor(
+                out=result[:, cols],
+                in0=change[:, cols],
+                scalar=gate[:],
+                in1=before_sb[:, cols],
+                op0=ALU.mult,
+                op1=ALU.add,
+            )
+            queue.dma_start(out=out[:, cols], in_=result[:, cols])

@@ -30,18 +30,17 @@ def tile_attend_lookahead_dampened_movedbychange_kernel(
     nc = tc.nc
     with ExitStack() as ctx:
         sb = ctx.enter_context(tc.tile_pool(name="sb", bufs=1))
-        acc = ctx.enter_context(tc.psum_pool(name="acc", bufs=4))
-        turn = ctx.enter_context(tc.psum_pool(name="turn", bufs=4))
+        ps = ctx.enter_context(tc.psum_pool(name="ps", bufs=1))
 
         k_scales = sb.tile([P, BANK], U8, align_bytes=64)
-        nc.vector.memset(k_scales[:].bitcast(I32), 0)
+        nc.gpsimd.memset(k_scales[:].bitcast(I32), 0)
+        q_raw = sb.tile([P, PACK, Q], F32)
+        nc.sync.dma_start(out=q_raw[:], in_=query.rearrange("(p j) q -> p j q", j=PACK))
         for quad in range(4):
             nc.sync.dma_start(
                 out=k_scales[32 * quad : 32 * quad + 16, :].bitcast(I32),
                 in_=keys_scales[0, 4 * quad : 4 * quad + 4, :].rearrange("r (c n) -> c r n", c=CHUNKS).bitcast(I32),
             )
-        q_raw = sb.tile([P, PACK, Q], F32)
-        nc.sync.dma_start(out=q_raw[:], in_=query.rearrange("(p j) q -> p j q", j=PACK))
         key_bytes = keys_words[0].rearrange("p n t -> p (n t)")
         k_codes = []
         for c in range(CHUNKS):
@@ -56,19 +55,20 @@ def tile_attend_lookahead_dampened_movedbychange_kernel(
         nc.sync.dma_start(list3[:], offs3)
         list1 = sb.tile([P, I // 16], U16)
         nc.sync.dma_start(list1[:], offs)
-        os_col = sb.tile([P, PACK], F32)
+        factor_cols = sb.tile([P, PACK], F32)
         lam_sb = sb.tile([P, 1], F32)
         damp_sb = sb.tile([P, 1], F32)
         eager_sb = sb.tile([P, 1], F32)
+        nc.sync.dma_start(out=lam_sb[:], in_=lam)
         small_after = (
-            ((lam_sb, lam),),
-            ((damp_sb, damp), (os_col, slot_factor.rearrange("o (p t) -> p (o t)", t=PACK))),
+            ((damp_sb, damp),),
+            ((factor_cols, slot_factor.rearrange("o (p t) -> p (o t)", t=PACK)),),
             ((eager_sb, eager2),),
             (),
         )
         v_pool = []
         for b in range(BLOCKS):
-            pool_rows = sb.tile([P, T], F32, name="v_pool%d" % b)
+            pool_rows = sb.tile([P, T], F32, tag="values%d" % b, name="pool_rows", align_bytes=64)
             nc.sync.dma_start(out=pool_rows[:], in_=vals[b * P : (b + 1) * P, :])
             v_pool.append(pool_rows)
             for small, source in small_after[b]:
@@ -79,50 +79,84 @@ def tile_attend_lookahead_dampened_movedbychange_kernel(
         ident = sb.tile([P, P], F32)
         make_identity(nc, ident[:])
 
-        q_bf = sb.tile([P, Q, PACK], BF16, align_bytes=64)
-        nc.vector.tensor_copy(out=q_bf[:], in_=q_raw[:].rearrange("p j q -> p q j"))
+        q_bf = sb.tile([P, Q * PACK], BF16, align_bytes=64)
         q_codes = sb.tile([P, Q], U32, align_bytes=64)
         q_scales = sb.tile([P, Q], U8, align_bytes=64)
-        nc.vector.quantize_mx(
-            out=q_codes[:].bitcast(FP8X4), scales=q_scales[:], in_=q_bf[:].rearrange("p q j -> p (q j)")
-        )
+        for lo in range(0, Q, Q // 2):
+            nc.vector.tensor_copy(
+                out=q_bf[:, lo * PACK : (lo + Q // 2) * PACK].rearrange("p (q j) -> p q j", j=PACK),
+                in_=q_raw[:, :, lo : lo + Q // 2].rearrange("p j q -> p q j"),
+            )
+        for lo in range(0, Q, Q // 2):
+            nc.vector.quantize_mx(
+                out=q_codes[:, lo : lo + Q // 2].bitcast(FP8X4),
+                scales=q_scales[:, lo : lo + Q // 2],
+                in_=q_bf[:, lo * PACK : (lo + Q // 2) * PACK],
+            )
 
-        a_sb = sb.tile([P, T], F32)
-        for c in range(CHUNKS):
-            a_ps = acc.tile([P, BANK], F32, tag="acc", name="a_ps")
+        a_sb = sb.tile([P, T], F32, tag="a_then_picked0", align_bytes=64)
+        pieces = ((0, 0, BANK), (1, 0, BANK), (2, 0, BANK), (3, 0, BANK // 2), (3, BANK // 2, BANK))
+        for n, (c, lo, hi) in enumerate(pieces):
+            a_ps = ps.tile([P, hi - lo], F32, tag="bank%d" % n, name="a_ps")
             nc.tensor.matmul_mx(
                 out=a_ps[:],
                 lhsT=q_codes[:].bitcast(FP8X4),
                 lhsT_scale=q_scales[:],
-                rhs=k_codes[c][:].bitcast(FP8X4),
-                rhs_scale=k_scales[4 * c : P, :],
+                rhs=k_codes[c][:, lo:hi].bitcast(FP8X4),
+                rhs_scale=k_scales[4 * c : P, lo:hi],
                 start=True,
                 stop=True,
             )
-            cols = slice(c * BANK, (c + 1) * BANK)
-            if c % 2 == 0:
-                nc.vector.tensor_copy(out=a_sb[:, cols], in_=a_ps[:])
-            else:
-                nc.scalar.copy(out=a_sb[:, cols], in_=a_ps[:])
+            copy = nc.vector.tensor_copy if n % 2 == 0 else nc.scalar.copy
+            copy(out=a_sb[:, c * BANK + lo : c * BANK + hi], in_=a_ps[:])
 
         a2 = sb.tile([P, I], F32)
         nc.scalar.activation(a2[:], a_sb[:].indirect(list2[:]), ACT.Copy)
         a3 = sb.tile([P, I], F32)
         nc.vector.tensor_copy(a3[:], a_sb[:].indirect(list3[:]))
         a1 = sb.tile([P, I], F32)
-        nc.scalar.activation(a1[:], a_sb[:].indirect(list1[:]), ACT.Copy)
+        cut = 3 * I // 4
+        nc.scalar.activation(a1[:, :cut], a_sb[:].indirect(list1[:, : cut // 16]), ACT.Copy)
+        nc.vector.tensor_copy(a1[:, cut:], a_sb[:].indirect(list1[:, cut // 16 :]))
         follower = sb.tile([P, I], F32)
         nc.vector.tensor_tensor(out=follower[:], in0=a2[:], in1=a3[:], op=ALU.max)
-        score = sb.tile([P, I], F32)
+        score = sb.tile([P, I], F32, tag="score_then_picked1", align_bytes=64)
         nc.vector.scalar_tensor_tensor(
             out=score[:], in0=follower[:], scalar=lam_sb[:], in1=a1[:], op0=ALU.mult, op1=ALU.add
         )
+        neg_score = sb.tile([P, I], F32)
         neg_max = sb.tile([P, 1], F32)
-        nc.vector.tensor_reduce(out=neg_max[:], in_=score[:], axis=AXIS.X, op=ALU.max, negate=True)
-        p_sb = sb.tile([P, I], F32)
+        nc.vector.tensor_scalar(
+            out=neg_score[:], in0=score[:], scalar1=-1.0, scalar2=None, op0=ALU.mult, op1=ALU.min, accum_out=neg_max[:]
+        )
+
+        def turn(rows_bf, turned):
+            words = rows_bf[:].bitcast(F32)
+            for u in range(2):
+                nc.tensor.transpose(turned[:, u, :], words[:, u : I // 2 : 2], ident[:])
+
+        def interleave(copy, grouped, turned):
+            copy(
+                out=grouped.bitcast(F32).rearrange("p (b r u) -> p b r u", r=P, u=2),
+                in_=turned.rearrange("p b u r -> p b r u"),
+            )
+
+        turned01 = ps.tile([P, 2, 2, P], F32, tag="bank6")
+        picked0 = sb.tile([P, I], BF16, tag="a_then_picked0", align_bytes=64)
+        nc.scalar.activation(picked0[:], v_pool[0][:].indirect(list1[:]), ACT.Copy)
+        turn(picked0, turned01[:, 0])
+
+        p_sb = sb.tile([P, I], F32, tag="values0", align_bytes=64)
         p_sum = sb.tile([P, 1], F32)
-        nc.scalar.activation(out=p_sb[:], in_=score[:], func=ACT.Exp, bias=neg_max[:], accum_out=p_sum[:])
-        p_inv = sb.tile([P, 1], F32)
+        nc.scalar.activation(
+            out=p_sb[:], in_=neg_score[:], func=ACT.Exp, bias=neg_max[:], scale=-1.0, accum_out=p_sum[:]
+        )
+
+        picked1 = sb.tile([P, I], BF16, tag="score_then_picked1", align_bytes=64)
+        nc.vector.tensor_copy(picked1[:], v_pool[1][:].indirect(list1[:]))
+        turn(picked1, turned01[:, 1])
+
+        p_inv = sb.tile([P, 1], F32, tag="values1", align_bytes=64)
         nc.vector.reciprocal(out=p_inv[:], in_=p_sum[:])
         gain = sb.tile([P, 1], F32)
         nc.vector.tensor_scalar(
@@ -131,55 +165,58 @@ def tile_attend_lookahead_dampened_movedbychange_kernel(
         part = sb.tile([P, I], F32)
         part_sum = sb.tile([P, 1], F32)
         nc.scalar.activation(out=part[:], in_=p_sb[:], func=ACT.Ln, bias=1.0, scale=gain[:], accum_out=part_sum[:])
-        part_inv = sb.tile([P, 1], F32)
+
+        picked2 = sb.tile([P, I], BF16, tag="values1", align_bytes=64)
+        nc.vector.tensor_copy(picked2[:], v_pool[2][:].indirect(list1[:]))
+        turned2 = ps.tile([P, 1, 2, P], F32, tag="bank7")
+        turn(picked2, turned2[:, 0])
+
+        block = P * PACK
+        grouped01 = sb.tile([P, 2 * block], BF16, tag="values2", align_bytes=64)
+        interleave(nc.vector.tensor_copy, grouped01[:], turned01[:])
+
+        part_inv = sb.tile([P, 1], F32, tag="values1", align_bytes=64)
         nc.vector.reciprocal(out=part_inv[:], in_=part_sum[:])
 
-        os_ps = turn.tile([P, PACK, P], F32, tag="turn", name="os_ps")
+        factor_rows = ps.tile([P, PACK, P], F32, tag="bank5")
         for t in range(PACK):
-            nc.tensor.transpose(os_ps[:, t, :], os_col[:, t : t + 1].to_broadcast([P, P]), ident[:])
-        os_rows = sb.tile([P, P, PACK], F32)
-        nc.scalar.copy(out=os_rows[:], in_=os_ps[:].rearrange("q t p -> q p t"))
+            nc.tensor.transpose(factor_rows[:, t, :], factor_cols[:, t : t + 1].to_broadcast([P, P]), ident[:])
 
-        w_bf = sb.tile([P, I], BF16)
-        nc.vector.scalar_tensor_tensor(
-            out=w_bf[:],
-            in0=part[:],
-            scalar=part_inv[:],
-            in1=os_rows[:].rearrange("q p t -> q (p t)"),
-            op0=ALU.mult,
-            op1=ALU.mult,
-        )
-
-        def turn_and_quantise(rows_bf, name, copy, codes, scales):
-            words = rows_bf[:].bitcast(F32)
-            turned = turn.tile([P, 2, P], F32, tag="turn", name="turned")
-            for u in range(2):
-                nc.tensor.transpose(turned[:, u, :], words[:, u : I // 2 : 2], ident[:])
-            grouped = sb.tile([P, P * PACK], BF16, name=name, align_bytes=64)
-            copy(
-                out=grouped[:].bitcast(F32).rearrange("p (r u) -> p r u", u=2),
-                in_=turned[:].rearrange("p u r -> p r u"),
+        w_bf = sb.tile([P, 2, P, 2], BF16)
+        turned_w = ps.tile([P, 1, 2, P], F32, tag="bank0")
+        for u in range(2):
+            nc.vector.scalar_tensor_tensor(
+                out=w_bf[:, u],
+                in0=part[:].rearrange("q (p t) -> q p t", t=PACK)[:, :, 2 * u : 2 * u + 2],
+                scalar=part_inv[:],
+                in1=factor_rows[:, 2 * u : 2 * u + 2, :].rearrange("q t p -> q p t"),
+                op0=ALU.mult,
+                op1=ALU.mult,
             )
-            nc.vector.quantize_mx(out=codes.bitcast(FP8X4), scales=scales, in_=grouped[:])
+            nc.tensor.transpose(
+                turned_w[:, 0, u, :], w_bf[:, u].rearrange("q p h -> q (p h)").bitcast(F32), ident[:]
+            )
 
+        picked3 = sb.tile([P, I], BF16, tag="values0", align_bytes=64)
+        nc.scalar.activation(picked3[:], v_pool[3][:].indirect(list1[:]), ACT.Copy)
+        turned3 = ps.tile([P, 1, 2, P], F32, tag="bank1")
+        turn(picked3, turned3[:, 0])
+
+        w_grouped = sb.tile([P, Q * PACK], BF16, align_bytes=64)
+        interleave(nc.vector.tensor_copy, w_grouped[:], turned_w[:])
         w_codes = sb.tile([P, Q], U32, align_bytes=64)
         w_scales = sb.tile([P, Q], U8, align_bytes=64)
-        turn_and_quantise(w_bf, "w_grouped", nc.scalar.copy, w_codes[:], w_scales[:])
+        nc.vector.quantize_mx(out=w_codes[:].bitcast(FP8X4), scales=w_scales[:], in_=w_grouped[:])
 
         v_codes = sb.tile([P, E], U32, align_bytes=64)
         v_scales = sb.tile([P, E], U8, align_bytes=64)
-        half = I // 2
-        for b in range(BLOCKS):
-            picked = sb.tile([P, I], BF16, name="picked%d" % b)
-            if b == 0:
-                nc.scalar.activation(picked[:], v_pool[b][:].indirect(list1[:]), ACT.Copy)
-            elif b < BLOCKS - 1:
-                nc.vector.tensor_copy(picked[:], v_pool[b][:].indirect(list1[:]))
-            else:
-                nc.vector.tensor_copy(picked[:, :half], v_pool[b][:].indirect(list1[:, : half // 16]))
-                nc.scalar.activation(picked[:, half:], v_pool[b][:].indirect(list1[:, half // 16 :]), ACT.Copy)
+        nc.vector.quantize_mx(out=v_codes[:, : 2 * P].bitcast(FP8X4), scales=v_scales[:, : 2 * P], in_=grouped01[:])
+        grouped23 = sb.tile([P, 2 * block], BF16, tag="values3", align_bytes=64)
+        for b, turned in ((2, turned2), (3, turned3)):
+            grouped = grouped23[:, (b - 2) * block : (b - 1) * block]
+            interleave(nc.scalar.copy, grouped, turned[:])
             cols = slice(b * P, (b + 1) * P)
-            turn_and_quantise(picked, "v_grouped%d" % b, nc.vector.tensor_copy, v_codes[:, cols], v_scales[:, cols])
+            nc.vector.quantize_mx(out=v_codes[:, cols].bitcast(FP8X4), scales=v_scales[:, cols], in_=grouped)
 
         def second_product(o_out, cols):
             nc.tensor.matmul_mx(
@@ -192,29 +229,27 @@ def tile_attend_lookahead_dampened_movedbychange_kernel(
                 stop=True,
             )
 
-        early = E - P
-        o_early = acc.tile([P, early], F32, tag="acc", name="o_early")
-        second_product(o_early[:, : 2 * P], slice(0, 2 * P))
-        second_product(o_early[:, 2 * P :], slice(2 * P, early))
-        o_late = acc.tile([P, P], F32, tag="acc", name="o_late")
-        second_product(o_late[:], slice(early, E))
-
-        eager_mean = sb.tile([P, 1], F32)
-        nc.vector.tensor_scalar(out=eager_mean[:], in0=eager_sb[:], scalar1=1.0 / E, scalar2=None, op0=ALU.mult)
         change = sb.tile([P, E], F32)
+        for h in range(2):
+            cols = slice(h * E // 2, (h + 1) * E // 2)
+            o_ps = ps.tile([P, E // 2], F32, tag="bank%d" % (3 + h), name="o_ps")
+            second_product(o_ps[:], cols)
+            nc.vector.tensor_tensor(out=change[:, cols], in0=o_ps[:], in1=before_sb[:, cols], op=ALU.subtract)
         squares = sb.tile([P, E], F32)
-        sum_early = sb.tile([P, 1], F32)
-        sum_late = sb.tile([P, 1], F32)
-        nc.vector.tensor_tensor(out=change[:, :early], in0=o_early[:], in1=before_sb[:, :early], op=ALU.subtract)
-        nc.scalar.activation(out=squares[:, :early], in_=change[:, :early], func=ACT.Square, accum_out=sum_early[:])
-        nc.vector.tensor_tensor(out=change[:, early:], in0=o_late[:], in1=before_sb[:, early:], op=ALU.subtract)
-        nc.scalar.activation(out=squares[:, early:], in_=change[:, early:], func=ACT.Square, accum_out=sum_late[:])
-        gate_bias = sb.tile([P, 1], F32)
-        nc.vector.tensor_scalar(
-            out=gate_bias[:], in0=sum_early[:], scalar1=eager_mean[:], scalar2=-1.0, op0=ALU.mult, op1=ALU.add
+        mean_square = sb.tile([P, 1], F32)
+        nc.vector.scalar_tensor_tensor(
+            out=squares[:],
+            in0=change[:],
+            scalar=1.0 / E,
+            in1=change[:],
+            op0=ALU.mult,
+            op1=ALU.mult,
+            accum_out=mean_square[:],
         )
+        minus_one = sb.tile([P, 1], F32)
+        nc.gpsimd.memset(minus_one[:], -1.0)
         gate = sb.tile([P, 1], F32)
-        nc.scalar.activation(out=gate[:], in_=sum_late[:], func=ACT.Sigmoid, bias=gate_bias[:], scale=eager_mean[:])
+        nc.scalar.activation(out=gate[:], in_=mean_square[:], func=ACT.Sigmoid, bias=minus_one[:], scale=eager_sb[:])
         result = sb.tile([P, E], F32)
         for h, queue in enumerate((nc.sync, nc.scalar)):
             cols = slice(h * E // 2, (h + 1) * E // 2)

@@ -42,11 +42,12 @@ def tile_attend_lookahead_dampened_movedbychange_kernel(
                 in_=keys_scales[0, 4 * quad : 4 * quad + 4, :].rearrange("r (c n) -> c r n", c=CHUNKS).bitcast(I32),
             )
         key_bytes = keys_words[0].rearrange("p n t -> p (n t)")
+        pieces = ((0, 0, BANK), (1, 0, BANK), (2, 0, BANK), (3, 0, BANK // 2), (3, BANK // 2, BANK))
         k_codes = []
-        for c in range(CHUNKS):
-            codes = sb.tile([P, BANK], U32, name="k_codes%d" % c, align_bytes=64)
+        for n, (c, lo, hi) in enumerate(pieces):
+            codes = sb.tile([P, hi - lo], U32, name="k_codes%d" % n, align_bytes=64)
             nc.sync.dma_start(
-                out=codes[:].bitcast(I32), in_=key_bytes[:, c * BANK * PACK : (c + 1) * BANK * PACK].bitcast(I32)
+                out=codes[:].bitcast(I32), in_=key_bytes[:, (c * BANK + lo) * PACK : (c * BANK + hi) * PACK].bitcast(I32)
             )
             k_codes.append(codes)
         list2 = sb.tile([P, I // 16], U16)
@@ -94,15 +95,14 @@ def tile_attend_lookahead_dampened_movedbychange_kernel(
                 in_=q_bf[:, lo * PACK : (lo + Q // 2) * PACK],
             )
 
-        a_sb = sb.tile([P, T], F32, tag="a_then_picked0", align_bytes=64)
-        pieces = ((0, 0, BANK), (1, 0, BANK), (2, 0, BANK), (3, 0, BANK // 2), (3, BANK // 2, BANK))
+        a_sb = sb.tile([P, T], F32)
         for n, (c, lo, hi) in enumerate(pieces):
             a_ps = ps.tile([P, hi - lo], F32, tag="bank%d" % n, name="a_ps")
             nc.tensor.matmul_mx(
                 out=a_ps[:],
                 lhsT=q_codes[:].bitcast(FP8X4),
                 lhsT_scale=q_scales[:],
-                rhs=k_codes[c][:, lo:hi].bitcast(FP8X4),
+                rhs=k_codes[n][:].bitcast(FP8X4),
                 rhs_scale=k_scales[4 * c : P, lo:hi],
                 start=True,
                 stop=True,
@@ -115,15 +115,19 @@ def tile_attend_lookahead_dampened_movedbychange_kernel(
         a3 = sb.tile([P, I], F32)
         nc.vector.tensor_copy(a3[:], a_sb[:].indirect(list3[:]))
         a1 = sb.tile([P, I], F32)
-        cut = 3 * I // 4
-        nc.scalar.activation(a1[:, :cut], a_sb[:].indirect(list1[:, : cut // 16]), ACT.Copy)
+        half, cut = I // 2, 3 * I // 4
+        for lo, hi in ((0, half), (half, cut)):
+            nc.scalar.activation(a1[:, lo:hi], a_sb[:].indirect(list1[:, lo // 16 : hi // 16]), ACT.Copy)
         nc.vector.tensor_copy(a1[:, cut:], a_sb[:].indirect(list1[:, cut // 16 :]))
         follower = sb.tile([P, I], F32)
-        nc.vector.tensor_tensor(out=follower[:], in0=a2[:], in1=a3[:], op=ALU.max)
-        score = sb.tile([P, I], F32, tag="score_then_picked1", align_bytes=64)
-        nc.vector.scalar_tensor_tensor(
-            out=score[:], in0=follower[:], scalar=lam_sb[:], in1=a1[:], op0=ALU.mult, op1=ALU.add
-        )
+        score = sb.tile([P, I], F32)
+        halves = (slice(0, half), slice(half, I))
+        for cols in halves:
+            nc.vector.tensor_tensor(out=follower[:, cols], in0=a2[:, cols], in1=a3[:, cols], op=ALU.max)
+        for cols in halves:
+            nc.vector.scalar_tensor_tensor(
+                out=score[:, cols], in0=follower[:, cols], scalar=lam_sb[:], in1=a1[:, cols], op0=ALU.mult, op1=ALU.add
+            )
         neg_score = sb.tile([P, I], F32)
         neg_max = sb.tile([P, 1], F32)
         nc.vector.tensor_scalar(
@@ -142,7 +146,7 @@ def tile_attend_lookahead_dampened_movedbychange_kernel(
             )
 
         turned01 = ps.tile([P, 2, 2, P], F32, tag="bank6")
-        picked0 = sb.tile([P, I], BF16, tag="a_then_picked0", align_bytes=64)
+        picked0 = sb.tile([P, I], BF16)
         nc.scalar.activation(picked0[:], v_pool[0][:].indirect(list1[:]), ACT.Copy)
         turn(picked0, turned01[:, 0])
 
@@ -152,7 +156,7 @@ def tile_attend_lookahead_dampened_movedbychange_kernel(
             out=p_sb[:], in_=neg_score[:], func=ACT.Exp, bias=neg_max[:], scale=-1.0, accum_out=p_sum[:]
         )
 
-        picked1 = sb.tile([P, I], BF16, tag="score_then_picked1", align_bytes=64)
+        picked1 = sb.tile([P, I], BF16)
         nc.vector.tensor_copy(picked1[:], v_pool[1][:].indirect(list1[:]))
         turn(picked1, turned01[:, 1])
 
@@ -162,20 +166,17 @@ def tile_attend_lookahead_dampened_movedbychange_kernel(
         nc.vector.tensor_scalar(
             out=gain[:], in0=p_inv[:], scalar1=damp_sb[:], scalar2=float(I), op0=ALU.mult, op1=ALU.mult
         )
-        part = sb.tile([P, I], F32)
+        part = sb.tile([P, I], F32, tag="part_then_grouped01", align_bytes=64)
         part_sum = sb.tile([P, 1], F32)
         nc.scalar.activation(out=part[:], in_=p_sb[:], func=ACT.Ln, bias=1.0, scale=gain[:], accum_out=part_sum[:])
 
-        picked2 = sb.tile([P, I], BF16, tag="values1", align_bytes=64)
+        picked2 = sb.tile([P, I], BF16)
         nc.vector.tensor_copy(picked2[:], v_pool[2][:].indirect(list1[:]))
         turned2 = ps.tile([P, 1, 2, P], F32, tag="bank7")
         turn(picked2, turned2[:, 0])
 
         block = P * PACK
-        grouped01 = sb.tile([P, 2 * block], BF16, tag="values2", align_bytes=64)
-        interleave(nc.vector.tensor_copy, grouped01[:], turned01[:])
-
-        part_inv = sb.tile([P, 1], F32, tag="values1", align_bytes=64)
+        part_inv = sb.tile([P, 1], F32, tag="values2", align_bytes=64)
         nc.vector.reciprocal(out=part_inv[:], in_=part_sum[:])
 
         factor_rows = ps.tile([P, PACK, P], F32, tag="bank5")
@@ -197,11 +198,13 @@ def tile_attend_lookahead_dampened_movedbychange_kernel(
                 turned_w[:, 0, u, :], w_bf[:, u].rearrange("q p h -> q (p h)").bitcast(F32), ident[:]
             )
 
-        picked3 = sb.tile([P, I], BF16, tag="values0", align_bytes=64)
+        picked3 = sb.tile([P, I], BF16)
         nc.scalar.activation(picked3[:], v_pool[3][:].indirect(list1[:]), ACT.Copy)
-        turned3 = ps.tile([P, 1, 2, P], F32, tag="bank1")
+        turned3 = ps.tile([P, 1, 2, P], F32, tag="bank5")
         turn(picked3, turned3[:, 0])
 
+        grouped01 = sb.tile([P, 2 * block], BF16, tag="part_then_grouped01", align_bytes=64)
+        interleave(nc.vector.tensor_copy, grouped01[:], turned01[:])
         w_grouped = sb.tile([P, Q * PACK], BF16, align_bytes=64)
         interleave(nc.vector.tensor_copy, w_grouped[:], turned_w[:])
         w_codes = sb.tile([P, Q], U32, align_bytes=64)
@@ -230,11 +233,14 @@ def tile_attend_lookahead_dampened_movedbychange_kernel(
             )
 
         change = sb.tile([P, E], F32)
-        for h in range(2):
-            cols = slice(h * E // 2, (h + 1) * E // 2)
-            o_ps = ps.tile([P, E // 2], F32, tag="bank%d" % (3 + h), name="o_ps")
-            second_product(o_ps[:], cols)
-            nc.vector.tensor_tensor(out=change[:, cols], in0=o_ps[:], in1=before_sb[:, cols], op=ALU.subtract)
+        early = 3 * P
+        o_early = ps.tile([P, early], F32, tag="bank3")
+        second_product(o_early[:, 2 * P :], slice(2 * P, early))
+        second_product(o_early[:, : 2 * P], slice(0, 2 * P))
+        o_late = ps.tile([P, P], F32, tag="bank4")
+        second_product(o_late[:], slice(early, E))
+        nc.vector.tensor_tensor(out=change[:, :early], in0=o_early[:], in1=before_sb[:, :early], op=ALU.subtract)
+        nc.vector.tensor_tensor(out=change[:, early:], in0=o_late[:], in1=before_sb[:, early:], op=ALU.subtract)
         squares = sb.tile([P, E], F32)
         mean_square = sb.tile([P, 1], F32)
         nc.vector.scalar_tensor_tensor(

@@ -15,13 +15,19 @@ U8 = mybir.dt.uint8
 FP8X4 = mybir.dt.float8_e4m3fn_x4
 ALU = mybir.AluOpType
 ACT = mybir.ActivationFunctionType
-AXIS = mybir.AxisListType
 
 P = 128
 PACK = 4
+PAIRS = 2
+QUADRANT = 32
+SCALE_ROWS = 4
+LIST_ROWS = 16
 BANK = 512
 CHUNKS = T // BANK
 BLOCKS = E // P
+GROUPED = P * PACK
+SLOT_HALF = I // 2
+SCALAR_SLOTS = 3 * I // 4
 
 
 def tile_attend_lookahead_dampened_movedbychange_kernel(
@@ -35,98 +41,114 @@ def tile_attend_lookahead_dampened_movedbychange_kernel(
         k_scales = sb.tile([P, BANK], U8, align_bytes=64)
         nc.gpsimd.memset(k_scales[:].bitcast(I32), 0)
         q_raw = sb.tile([P, PACK, Q], F32)
-        nc.sync.dma_start(out=q_raw[:], in_=query.rearrange("(p j) q -> p j q", j=PACK))
-        for quad in range(4):
+        nc.sync.dma_start(out=q_raw[:], in_=query.rearrange("(p t) q -> p t q", t=PACK))
+        for quad in range(P // QUADRANT):
+            scale_rows = keys_scales[0, SCALE_ROWS * quad : SCALE_ROWS * (quad + 1), :]
             nc.sync.dma_start(
-                out=k_scales[32 * quad : 32 * quad + 16, :].bitcast(I32),
-                in_=keys_scales[0, 4 * quad : 4 * quad + 4, :].rearrange("r (c n) -> c r n", c=CHUNKS).bitcast(I32),
+                out=k_scales[QUADRANT * quad : QUADRANT * quad + CHUNKS * SCALE_ROWS, :].bitcast(I32),
+                in_=scale_rows.rearrange("r (c n) -> c r n", c=CHUNKS).bitcast(I32),
             )
         key_bytes = keys_words[0].rearrange("p n t -> p (n t)")
-        pieces = ((0, 0, BANK), (1, 0, BANK), (2, 0, BANK), (3, 0, BANK // 2), (3, BANK // 2, BANK))
         k_codes = []
-        for n, (c, lo, hi) in enumerate(pieces):
-            codes = sb.tile([P, hi - lo], U32, name="k_codes%d" % n, align_bytes=64)
+        for c in range(CHUNKS):
+            chunk_codes = sb.tile([P, BANK], U32, name="k_codes%d" % c, align_bytes=64)
             nc.sync.dma_start(
-                out=codes[:].bitcast(I32), in_=key_bytes[:, (c * BANK + lo) * PACK : (c * BANK + hi) * PACK].bitcast(I32)
+                out=chunk_codes[:].bitcast(I32),
+                in_=key_bytes[:, c * BANK * PACK : (c + 1) * BANK * PACK].bitcast(I32),
             )
-            k_codes.append(codes)
-        list2 = sb.tile([P, I // 16], U16)
+            k_codes.append(chunk_codes)
+        list2 = sb.tile([P, I // LIST_ROWS], U16)
         nc.sync.dma_start(list2[:], offs2)
-        list3 = sb.tile([P, I // 16], U16)
+        list3 = sb.tile([P, I // LIST_ROWS], U16)
         nc.sync.dma_start(list3[:], offs3)
-        list1 = sb.tile([P, I // 16], U16)
+        list1 = sb.tile([P, I // LIST_ROWS], U16)
         nc.sync.dma_start(list1[:], offs)
+
+        def load_values(b):
+            value_rows = sb.tile([P, T], F32, tag="values%d" % b, name="value_rows", align_bytes=64)
+            nc.sync.dma_start(out=value_rows[:], in_=vals[b * P : (b + 1) * P, :])
+            return value_rows
+
         factor_cols = sb.tile([P, PACK], F32)
         lam_sb = sb.tile([P, 1], F32)
         damp_sb = sb.tile([P, 1], F32)
         eager_sb = sb.tile([P, 1], F32)
+        values0 = load_values(0)
         nc.sync.dma_start(out=lam_sb[:], in_=lam)
-        small_after = (
-            ((damp_sb, damp),),
-            ((factor_cols, slot_factor.rearrange("o (p t) -> p (o t)", t=PACK)),),
-            ((eager_sb, eager2),),
-            (),
-        )
-        v_pool = []
-        for b in range(BLOCKS):
-            pool_rows = sb.tile([P, T], F32, tag="values%d" % b, name="pool_rows", align_bytes=64)
-            nc.sync.dma_start(out=pool_rows[:], in_=vals[b * P : (b + 1) * P, :])
-            v_pool.append(pool_rows)
-            for small, source in small_after[b]:
-                nc.sync.dma_start(out=small[:], in_=source)
+        nc.sync.dma_start(out=damp_sb[:], in_=damp)
+        values1 = load_values(1)
+        nc.sync.dma_start(out=factor_cols[:], in_=slot_factor.rearrange("o (p t) -> p (o t)", t=PACK))
+        values2 = load_values(2)
+        nc.sync.dma_start(out=eager_sb[:], in_=eager2)
+        values3 = load_values(3)
         before_sb = sb.tile([P, E], F32)
         nc.sync.dma_start(out=before_sb[:], in_=before)
 
         ident = sb.tile([P, P], F32)
         make_identity(nc, ident[:])
 
-        q_bf = sb.tile([P, Q * PACK], BF16, align_bytes=64)
+        q_bf = sb.tile([P, GROUPED], BF16, align_bytes=64)
         q_codes = sb.tile([P, Q], U32, align_bytes=64)
         q_scales = sb.tile([P, Q], U8, align_bytes=64)
-        for lo in range(0, Q, Q // 2):
+        q_half = Q // 2
+        for first_row in range(0, Q, q_half):
             nc.vector.tensor_copy(
-                out=q_bf[:, lo * PACK : (lo + Q // 2) * PACK].rearrange("p (q j) -> p q j", j=PACK),
-                in_=q_raw[:, :, lo : lo + Q // 2].rearrange("p j q -> p q j"),
+                out=q_bf[:, first_row * PACK : (first_row + q_half) * PACK].rearrange("p (q t) -> p q t", t=PACK),
+                in_=q_raw[:, :, first_row : first_row + q_half].rearrange("p t q -> p q t"),
             )
-        for lo in range(0, Q, Q // 2):
+        for first_row in range(0, Q, q_half):
             nc.vector.quantize_mx(
-                out=q_codes[:, lo : lo + Q // 2].bitcast(FP8X4),
-                scales=q_scales[:, lo : lo + Q // 2],
-                in_=q_bf[:, lo * PACK : (lo + Q // 2) * PACK],
+                out=q_codes[:, first_row : first_row + q_half].bitcast(FP8X4),
+                scales=q_scales[:, first_row : first_row + q_half],
+                in_=q_bf[:, first_row * PACK : (first_row + q_half) * PACK],
             )
 
         a_sb = sb.tile([P, T], F32)
-        for n, (c, lo, hi) in enumerate(pieces):
-            a_ps = ps.tile([P, hi - lo], F32, tag="bank%d" % n, name="a_ps")
+        pieces = [(c, 0, BANK) for c in range(CHUNKS - 1)]
+        pieces.extend([(CHUNKS - 1, 0, BANK // 2), (CHUNKS - 1, BANK // 2, BANK)])
+        for n, (c, first_token, end_token) in enumerate(pieces):
+            a_ps = ps.tile([P, end_token - first_token], F32, tag="bank%d" % n, name="a_ps")
             nc.tensor.matmul_mx(
                 out=a_ps[:],
                 lhsT=q_codes[:].bitcast(FP8X4),
                 lhsT_scale=q_scales[:],
-                rhs=k_codes[n][:].bitcast(FP8X4),
-                rhs_scale=k_scales[4 * c : P, lo:hi],
+                rhs=k_codes[c][:, first_token:end_token].bitcast(FP8X4),
+                rhs_scale=k_scales[SCALE_ROWS * c : P, first_token:end_token],
                 start=True,
                 stop=True,
             )
-            copy = nc.vector.tensor_copy if n % 2 == 0 else nc.scalar.copy
-            copy(out=a_sb[:, c * BANK + lo : c * BANK + hi], in_=a_ps[:])
+            empty_bank = nc.vector.tensor_copy if n % 2 == 0 else nc.scalar.copy
+            empty_bank(out=a_sb[:, c * BANK + first_token : c * BANK + end_token], in_=a_ps[:])
+
+        def gather_on_scalar(gathered, window, entries, first_slot, end_slot):
+            listed = window[:].indirect(entries[:, first_slot // LIST_ROWS : end_slot // LIST_ROWS])
+            nc.scalar.activation(gathered[:, first_slot:end_slot], listed, ACT.Copy)
+
+        def gather_on_vector(gathered, window, entries, first_slot, end_slot):
+            listed = window[:].indirect(entries[:, first_slot // LIST_ROWS : end_slot // LIST_ROWS])
+            nc.vector.tensor_copy(gathered[:, first_slot:end_slot], listed)
 
         a2 = sb.tile([P, I], F32)
-        nc.scalar.activation(a2[:], a_sb[:].indirect(list2[:]), ACT.Copy)
+        gather_on_scalar(a2, a_sb, list2, 0, I)
         a3 = sb.tile([P, I], F32)
-        nc.vector.tensor_copy(a3[:], a_sb[:].indirect(list3[:]))
+        gather_on_vector(a3, a_sb, list3, 0, I)
         a1 = sb.tile([P, I], F32)
-        half, cut = I // 2, 3 * I // 4
-        for lo, hi in ((0, half), (half, cut)):
-            nc.scalar.activation(a1[:, lo:hi], a_sb[:].indirect(list1[:, lo // 16 : hi // 16]), ACT.Copy)
-        nc.vector.tensor_copy(a1[:, cut:], a_sb[:].indirect(list1[:, cut // 16 :]))
+        gather_on_scalar(a1, a_sb, list1, 0, SLOT_HALF)
+        gather_on_scalar(a1, a_sb, list1, SLOT_HALF, SCALAR_SLOTS)
+        gather_on_vector(a1, a_sb, list1, SCALAR_SLOTS, I)
         follower = sb.tile([P, I], F32)
         score = sb.tile([P, I], F32)
-        halves = (slice(0, half), slice(half, I))
-        for cols in halves:
-            nc.vector.tensor_tensor(out=follower[:, cols], in0=a2[:, cols], in1=a3[:, cols], op=ALU.max)
-        for cols in halves:
+        slot_halves = (slice(0, SLOT_HALF), slice(SLOT_HALF, I))
+        for slots in slot_halves:
+            nc.vector.tensor_tensor(out=follower[:, slots], in0=a2[:, slots], in1=a3[:, slots], op=ALU.max)
+        for slots in slot_halves:
             nc.vector.scalar_tensor_tensor(
-                out=score[:, cols], in0=follower[:, cols], scalar=lam_sb[:], in1=a1[:, cols], op0=ALU.mult, op1=ALU.add
+                out=score[:, slots],
+                in0=follower[:, slots],
+                scalar=lam_sb[:],
+                in1=a1[:, slots],
+                op0=ALU.mult,
+                op1=ALU.add,
             )
         neg_score = sb.tile([P, I], F32)
         neg_max = sb.tile([P, 1], F32)
@@ -134,21 +156,21 @@ def tile_attend_lookahead_dampened_movedbychange_kernel(
             out=neg_score[:], in0=score[:], scalar1=-1.0, scalar2=None, op0=ALU.mult, op1=ALU.min, accum_out=neg_max[:]
         )
 
-        def turn(rows_bf, turned):
-            words = rows_bf[:].bitcast(F32)
-            for u in range(2):
-                nc.tensor.transpose(turned[:, u, :], words[:, u : I // 2 : 2], ident[:])
+        def turn_picked(picked, turned):
+            pairs = picked[:].bitcast(F32)
+            for u in range(PAIRS):
+                nc.tensor.transpose(turned[:, u, :], pairs[:, u : SLOT_HALF : PAIRS], ident[:])
 
-        def interleave(copy, grouped, turned):
-            copy(
-                out=grouped.bitcast(F32).rearrange("p (b r u) -> p b r u", r=P, u=2),
+        def interleave(move, quantiser_input, turned):
+            move(
+                out=quantiser_input.bitcast(F32).rearrange("p (b r u) -> p b r u", r=P, u=PAIRS),
                 in_=turned.rearrange("p b u r -> p b r u"),
             )
 
-        turned01 = ps.tile([P, 2, 2, P], F32, tag="bank6")
+        turned01 = ps.tile([P, 2, PAIRS, P], F32, tag="bank6")
         picked0 = sb.tile([P, I], BF16)
-        nc.scalar.activation(picked0[:], v_pool[0][:].indirect(list1[:]), ACT.Copy)
-        turn(picked0, turned01[:, 0])
+        gather_on_scalar(picked0, values0, list1, 0, I)
+        turn_picked(picked0, turned01[:, 0])
 
         p_sb = sb.tile([P, I], F32, tag="values0", align_bytes=64)
         p_sum = sb.tile([P, 1], F32)
@@ -157,8 +179,8 @@ def tile_attend_lookahead_dampened_movedbychange_kernel(
         )
 
         picked1 = sb.tile([P, I], BF16)
-        nc.vector.tensor_copy(picked1[:], v_pool[1][:].indirect(list1[:]))
-        turn(picked1, turned01[:, 1])
+        gather_on_vector(picked1, values1, list1, 0, I)
+        turn_picked(picked1, turned01[:, 1])
 
         p_inv = sb.tile([P, 1], F32, tag="values1", align_bytes=64)
         nc.vector.reciprocal(out=p_inv[:], in_=p_sum[:])
@@ -166,16 +188,15 @@ def tile_attend_lookahead_dampened_movedbychange_kernel(
         nc.vector.tensor_scalar(
             out=gain[:], in0=p_inv[:], scalar1=damp_sb[:], scalar2=float(I), op0=ALU.mult, op1=ALU.mult
         )
-        part = sb.tile([P, I], F32, tag="part_then_grouped01", align_bytes=64)
+        part = sb.tile([P, I], F32)
         part_sum = sb.tile([P, 1], F32)
         nc.scalar.activation(out=part[:], in_=p_sb[:], func=ACT.Ln, bias=1.0, scale=gain[:], accum_out=part_sum[:])
 
         picked2 = sb.tile([P, I], BF16)
-        nc.vector.tensor_copy(picked2[:], v_pool[2][:].indirect(list1[:]))
-        turned2 = ps.tile([P, 1, 2, P], F32, tag="bank7")
-        turn(picked2, turned2[:, 0])
+        gather_on_vector(picked2, values2, list1, 0, I)
+        turned2 = ps.tile([P, 1, PAIRS, P], F32, tag="bank7")
+        turn_picked(picked2, turned2[:, 0])
 
-        block = P * PACK
         part_inv = sb.tile([P, 1], F32, tag="values2", align_bytes=64)
         nc.vector.reciprocal(out=part_inv[:], in_=part_sum[:])
 
@@ -183,9 +204,9 @@ def tile_attend_lookahead_dampened_movedbychange_kernel(
         for t in range(PACK):
             nc.tensor.transpose(factor_rows[:, t, :], factor_cols[:, t : t + 1].to_broadcast([P, P]), ident[:])
 
-        w_bf = sb.tile([P, 2, P, 2], BF16)
-        turned_w = ps.tile([P, 1, 2, P], F32, tag="bank0")
-        for u in range(2):
+        w_bf = sb.tile([P, PAIRS, P, 2], BF16)
+        turned_w = ps.tile([P, 1, PAIRS, P], F32, tag="bank0")
+        for u in range(PAIRS):
             nc.vector.scalar_tensor_tensor(
                 out=w_bf[:, u],
                 in0=part[:].rearrange("q (p t) -> q p t", t=PACK)[:, :, 2 * u : 2 * u + 2],
@@ -199,72 +220,68 @@ def tile_attend_lookahead_dampened_movedbychange_kernel(
             )
 
         picked3 = sb.tile([P, I], BF16)
-        nc.scalar.activation(picked3[:], v_pool[3][:].indirect(list1[:]), ACT.Copy)
-        turned3 = ps.tile([P, 1, 2, P], F32, tag="bank5")
-        turn(picked3, turned3[:, 0])
+        gather_on_scalar(picked3, values3, list1, 0, SCALAR_SLOTS)
+        gather_on_vector(picked3, values3, list1, SCALAR_SLOTS, I)
+        turned3 = ps.tile([P, 1, PAIRS, P], F32, tag="bank5")
+        turn_picked(picked3, turned3[:, 0])
 
-        grouped01 = sb.tile([P, 2 * block], BF16, tag="part_then_grouped01", align_bytes=64)
-        interleave(nc.vector.tensor_copy, grouped01[:], turned01[:])
-        w_grouped = sb.tile([P, Q * PACK], BF16, align_bytes=64)
-        interleave(nc.vector.tensor_copy, w_grouped[:], turned_w[:])
-        w_codes = sb.tile([P, Q], U32, align_bytes=64)
-        w_scales = sb.tile([P, Q], U8, align_bytes=64)
-        nc.vector.quantize_mx(out=w_codes[:].bitcast(FP8X4), scales=w_scales[:], in_=w_grouped[:])
-
+        grouped = sb.tile([P, (BLOCKS + 1) * GROUPED], BF16, tag="values3", align_bytes=64)
+        w_grouped = grouped[:, BLOCKS * GROUPED :]
+        interleave(nc.vector.tensor_copy, w_grouped, turned_w[:])
         v_codes = sb.tile([P, E], U32, align_bytes=64)
         v_scales = sb.tile([P, E], U8, align_bytes=64)
-        nc.vector.quantize_mx(out=v_codes[:, : 2 * P].bitcast(FP8X4), scales=v_scales[:, : 2 * P], in_=grouped01[:])
-        grouped23 = sb.tile([P, 2 * block], BF16, tag="values3", align_bytes=64)
-        for b, turned in ((2, turned2), (3, turned3)):
-            grouped = grouped23[:, (b - 2) * block : (b - 1) * block]
-            interleave(nc.scalar.copy, grouped, turned[:])
-            cols = slice(b * P, (b + 1) * P)
-            nc.vector.quantize_mx(out=v_codes[:, cols].bitcast(FP8X4), scales=v_scales[:, cols], in_=grouped)
+        w_codes = sb.tile([P, Q], U32, align_bytes=64)
+        w_scales = sb.tile([P, Q], U8, align_bytes=64)
+        nc.vector.quantize_mx(out=w_codes[:].bitcast(FP8X4), scales=w_scales[:], in_=w_grouped)
+        for first_block, end_block, turned_values in ((0, 2, turned01), (2, 3, turned2), (3, 4, turned3)):
+            v_grouped = grouped[:, first_block * GROUPED : end_block * GROUPED]
+            interleave(nc.scalar.copy, v_grouped, turned_values[:])
+            features = slice(first_block * P, end_block * P)
+            nc.vector.quantize_mx(out=v_codes[:, features].bitcast(FP8X4), scales=v_scales[:, features], in_=v_grouped)
 
-        def second_product(o_out, cols):
+        change = sb.tile([P, E], F32)
+        squares = sb.tile([P, E], F32)
+        feature_halves = (slice(0, E // 2), slice(E // 2, E))
+        mean_parts = []
+        for features, bank in zip(feature_halves, ("bank3", "bank4")):
+            o_ps = ps.tile([P, E // 2], F32, tag=bank, name="o_ps")
             nc.tensor.matmul_mx(
-                out=o_out,
+                out=o_ps[:],
                 lhsT=w_codes[:].bitcast(FP8X4),
                 lhsT_scale=w_scales[:],
-                rhs=v_codes[:, cols].bitcast(FP8X4),
-                rhs_scale=v_scales[:, cols],
+                rhs=v_codes[:, features].bitcast(FP8X4),
+                rhs_scale=v_scales[:, features],
                 start=True,
                 stop=True,
             )
-
-        change = sb.tile([P, E], F32)
-        early = 3 * P
-        o_early = ps.tile([P, early], F32, tag="bank3")
-        second_product(o_early[:, 2 * P :], slice(2 * P, early))
-        second_product(o_early[:, : 2 * P], slice(0, 2 * P))
-        o_late = ps.tile([P, P], F32, tag="bank4")
-        second_product(o_late[:], slice(early, E))
-        nc.vector.tensor_tensor(out=change[:, :early], in0=o_early[:], in1=before_sb[:, :early], op=ALU.subtract)
-        nc.vector.tensor_tensor(out=change[:, early:], in0=o_late[:], in1=before_sb[:, early:], op=ALU.subtract)
-        squares = sb.tile([P, E], F32)
-        mean_square = sb.tile([P, 1], F32)
-        nc.vector.scalar_tensor_tensor(
-            out=squares[:],
-            in0=change[:],
-            scalar=1.0 / E,
-            in1=change[:],
-            op0=ALU.mult,
-            op1=ALU.mult,
-            accum_out=mean_square[:],
-        )
-        minus_one = sb.tile([P, 1], F32)
-        nc.gpsimd.memset(minus_one[:], -1.0)
-        gate = sb.tile([P, 1], F32)
-        nc.scalar.activation(out=gate[:], in_=mean_square[:], func=ACT.Sigmoid, bias=minus_one[:], scale=eager_sb[:])
-        result = sb.tile([P, E], F32)
-        for h, queue in enumerate((nc.sync, nc.scalar)):
-            cols = slice(h * E // 2, (h + 1) * E // 2)
+            nc.vector.tensor_tensor(out=change[:, features], in0=o_ps[:], in1=before_sb[:, features], op=ALU.subtract)
+            mean_part = sb.tile([P, 1], F32, name="mean_part_" + bank)
             nc.vector.scalar_tensor_tensor(
-                out=result[:, cols],
-                in0=change[:, cols],
+                out=squares[:, features],
+                in0=change[:, features],
+                scalar=1.0 / E,
+                in1=change[:, features],
+                op0=ALU.mult,
+                op1=ALU.mult,
+                accum_out=mean_part[:],
+            )
+            mean_parts.append(mean_part)
+
+        gate_bias = sb.tile([P, 1], F32)
+        nc.vector.tensor_scalar(
+            out=gate_bias[:], in0=mean_parts[0][:], scalar1=eager_sb[:], scalar2=-1.0, op0=ALU.mult, op1=ALU.add
+        )
+        gate = sb.tile([P, 1], F32)
+        nc.scalar.activation(out=gate[:], in_=mean_parts[1][:], func=ACT.Sigmoid, bias=gate_bias[:], scale=eager_sb[:])
+
+        result = sb.tile([P, E], F32)
+        for features, queue in zip(feature_halves, (nc.sync, nc.scalar)):
+            nc.vector.scalar_tensor_tensor(
+                out=result[:, features],
+                in0=change[:, features],
                 scalar=gate[:],
-                in1=before_sb[:, cols],
+                in1=before_sb[:, features],
                 op0=ALU.mult,
                 op1=ALU.add,
             )
-            queue.dma_start(out=out[:, cols], in_=result[:, cols])
+            queue.dma_start(out=out[:, features], in_=result[:, features])

from contextlib import ExitStack

import concourse.mybir as mybir
from concourse.masks import make_identity

D, T, I, Q, E = 512, 2048, 512, 128, 512
FLOPS = 2 * D * Q * T + 2 * I * Q * E

F32 = mybir.dt.float32
BF16 = mybir.dt.bfloat16
I32 = mybir.dt.int32
U32 = mybir.dt.uint32
U16 = mybir.dt.uint16
U8 = mybir.dt.uint8
FP8X4 = mybir.dt.float8_e4m3fn_x4
ALU = mybir.AluOpType
ACT = mybir.ActivationFunctionType

P = 128
PACK = 4
PAIRS = 2
QUADRANT = 32
SCALE_ROWS = 4
LIST_ROWS = 16
BANK = 512
CHUNKS = T // BANK
BLOCKS = E // P
GROUPED = P * PACK
SLOT_HALF = I // 2
SCALAR_SLOTS = 3 * I // 4


def tile_attend_lookahead_dampened_movedbychange_kernel(
    tc, query, keys_words, keys_scales, lam, damp, slot_factor, vals, before, eager2, offs, offs2, offs3, out
):
    nc = tc.nc
    with ExitStack() as ctx:
        sb = ctx.enter_context(tc.tile_pool(name="sb", bufs=1))
        ps = ctx.enter_context(tc.psum_pool(name="ps", bufs=1))

        k_scales = sb.tile([P, BANK], U8, align_bytes=64)
        nc.gpsimd.memset(k_scales[:].bitcast(I32), 0)
        q_raw = sb.tile([P, PACK, Q], F32)
        nc.sync.dma_start(out=q_raw[:], in_=query.rearrange("(p t) q -> p t q", t=PACK))
        for quad in range(P // QUADRANT):
            scale_rows = keys_scales[0, SCALE_ROWS * quad : SCALE_ROWS * (quad + 1), :]
            nc.sync.dma_start(
                out=k_scales[QUADRANT * quad : QUADRANT * quad + CHUNKS * SCALE_ROWS, :].bitcast(I32),
                in_=scale_rows.rearrange("r (c n) -> c r n", c=CHUNKS).bitcast(I32),
            )
        key_bytes = keys_words[0].rearrange("p n t -> p (n t)")
        k_codes = []
        for c in range(CHUNKS):
            chunk_codes = sb.tile([P, BANK], U32, name="k_codes%d" % c, align_bytes=64)
            nc.sync.dma_start(
                out=chunk_codes[:].bitcast(I32),
                in_=key_bytes[:, c * BANK * PACK : (c + 1) * BANK * PACK].bitcast(I32),
            )
            k_codes.append(chunk_codes)
        list2 = sb.tile([P, I // LIST_ROWS], U16)
        nc.sync.dma_start(list2[:], offs2)
        list3 = sb.tile([P, I // LIST_ROWS], U16)
        nc.sync.dma_start(list3[:], offs3)
        list1 = sb.tile([P, I // LIST_ROWS], U16)
        nc.sync.dma_start(list1[:], offs)

        def load_values(b):
            value_rows = sb.tile([P, T], F32, tag="values%d" % b, name="value_rows", align_bytes=64)
            nc.sync.dma_start(out=value_rows[:], in_=vals[b * P : (b + 1) * P, :])
            return value_rows

        factor_cols = sb.tile([P, PACK], F32)
        lam_sb = sb.tile([P, 1], F32)
        damp_sb = sb.tile([P, 1], F32)
        eager_sb = sb.tile([P, 1], F32)
        values0 = load_values(0)
        nc.sync.dma_start(out=lam_sb[:], in_=lam)
        nc.sync.dma_start(out=damp_sb[:], in_=damp)
        values1 = load_values(1)
        nc.sync.dma_start(out=factor_cols[:], in_=slot_factor.rearrange("o (p t) -> p (o t)", t=PACK))
        values2 = load_values(2)
        nc.sync.dma_start(out=eager_sb[:], in_=eager2)
        values3 = load_values(3)
        before_sb = sb.tile([P, E], F32)
        nc.sync.dma_start(out=before_sb[:], in_=before)

        ident = sb.tile([P, P], F32)
        make_identity(nc, ident[:])

        q_bf = sb.tile([P, GROUPED], BF16, align_bytes=64)
        q_codes = sb.tile([P, Q], U32, align_bytes=64)
        q_scales = sb.tile([P, Q], U8, align_bytes=64)
        q_half = Q // 2
        for first_row in range(0, Q, q_half):
            nc.vector.tensor_copy(
                out=q_bf[:, first_row * PACK : (first_row + q_half) * PACK].rearrange("p (q t) -> p q t", t=PACK),
                in_=q_raw[:, :, first_row : first_row + q_half].rearrange("p t q -> p q t"),
            )
        for first_row in range(0, Q, q_half):
            nc.vector.quantize_mx(
                out=q_codes[:, first_row : first_row + q_half].bitcast(FP8X4),
                scales=q_scales[:, first_row : first_row + q_half],
                in_=q_bf[:, first_row * PACK : (first_row + q_half) * PACK],
            )

        a_sb = sb.tile([P, T], F32)
        pieces = [(c, 0, BANK) for c in range(CHUNKS - 1)]
        pieces.extend([(CHUNKS - 1, 0, BANK // 2), (CHUNKS - 1, BANK // 2, BANK)])
        for n, (c, first_token, end_token) in enumerate(pieces):
            a_ps = ps.tile([P, end_token - first_token], F32, tag="bank%d" % n, name="a_ps")
            nc.tensor.matmul_mx(
                out=a_ps[:],
                lhsT=q_codes[:].bitcast(FP8X4),
                lhsT_scale=q_scales[:],
                rhs=k_codes[c][:, first_token:end_token].bitcast(FP8X4),
                rhs_scale=k_scales[SCALE_ROWS * c : P, first_token:end_token],
                start=True,
                stop=True,
            )
            empty_bank = nc.vector.tensor_copy if n % 2 == 0 else nc.scalar.copy
            empty_bank(out=a_sb[:, c * BANK + first_token : c * BANK + end_token], in_=a_ps[:])

        def gather_on_scalar(gathered, window, entries, first_slot, end_slot):
            listed = window[:].indirect(entries[:, first_slot // LIST_ROWS : end_slot // LIST_ROWS])
            nc.scalar.activation(gathered[:, first_slot:end_slot], listed, ACT.Copy)

        def gather_on_vector(gathered, window, entries, first_slot, end_slot):
            listed = window[:].indirect(entries[:, first_slot // LIST_ROWS : end_slot // LIST_ROWS])
            nc.vector.tensor_copy(gathered[:, first_slot:end_slot], listed)

        a2 = sb.tile([P, I], F32)
        gather_on_scalar(a2, a_sb, list2, 0, I)
        a3 = sb.tile([P, I], F32)
        gather_on_vector(a3, a_sb, list3, 0, I)
        a1 = sb.tile([P, I], F32)
        gather_on_scalar(a1, a_sb, list1, 0, SLOT_HALF)
        gather_on_scalar(a1, a_sb, list1, SLOT_HALF, SCALAR_SLOTS)
        gather_on_vector(a1, a_sb, list1, SCALAR_SLOTS, I)
        follower = sb.tile([P, I], F32)
        score = sb.tile([P, I], F32)
        slot_halves = (slice(0, SLOT_HALF), slice(SLOT_HALF, I))
        for slots in slot_halves:
            nc.vector.tensor_tensor(out=follower[:, slots], in0=a2[:, slots], in1=a3[:, slots], op=ALU.max)
        for slots in slot_halves:
            nc.vector.scalar_tensor_tensor(
                out=score[:, slots],
                in0=follower[:, slots],
                scalar=lam_sb[:],
                in1=a1[:, slots],
                op0=ALU.mult,
                op1=ALU.add,
            )
        neg_score = sb.tile([P, I], F32)
        neg_max = sb.tile([P, 1], F32)
        nc.vector.tensor_scalar(
            out=neg_score[:], in0=score[:], scalar1=-1.0, scalar2=None, op0=ALU.mult, op1=ALU.min, accum_out=neg_max[:]
        )

        def turn_picked(picked, turned):
            pairs = picked[:].bitcast(F32)
            for u in range(PAIRS):
                nc.tensor.transpose(turned[:, u, :], pairs[:, u : SLOT_HALF : PAIRS], ident[:])

        def interleave(move, quantiser_input, turned):
            move(
                out=quantiser_input.bitcast(F32).rearrange("p (b r u) -> p b r u", r=P, u=PAIRS),
                in_=turned.rearrange("p b u r -> p b r u"),
            )

        turned01 = ps.tile([P, 2, PAIRS, P], F32, tag="bank6")
        picked0 = sb.tile([P, I], BF16)
        gather_on_scalar(picked0, values0, list1, 0, I)
        turn_picked(picked0, turned01[:, 0])

        p_sb = sb.tile([P, I], F32, tag="values0", align_bytes=64)
        p_sum = sb.tile([P, 1], F32)
        nc.scalar.activation(
            out=p_sb[:], in_=neg_score[:], func=ACT.Exp, bias=neg_max[:], scale=-1.0, accum_out=p_sum[:]
        )

        picked1 = sb.tile([P, I], BF16)
        gather_on_vector(picked1, values1, list1, 0, I)
        turn_picked(picked1, turned01[:, 1])

        p_inv = sb.tile([P, 1], F32, tag="values1", align_bytes=64)
        nc.vector.reciprocal(out=p_inv[:], in_=p_sum[:])
        gain = sb.tile([P, 1], F32)
        nc.vector.tensor_scalar(
            out=gain[:], in0=p_inv[:], scalar1=damp_sb[:], scalar2=float(I), op0=ALU.mult, op1=ALU.mult
        )
        part = sb.tile([P, I], F32)
        part_sum = sb.tile([P, 1], F32)
        nc.scalar.activation(out=part[:], in_=p_sb[:], func=ACT.Ln, bias=1.0, scale=gain[:], accum_out=part_sum[:])

        picked2 = sb.tile([P, I], BF16)
        gather_on_vector(picked2, values2, list1, 0, I)
        turned2 = ps.tile([P, 1, PAIRS, P], F32, tag="bank7")
        turn_picked(picked2, turned2[:, 0])

        part_inv = sb.tile([P, 1], F32, tag="values2", align_bytes=64)
        nc.vector.reciprocal(out=part_inv[:], in_=part_sum[:])

        factor_rows = ps.tile([P, PACK, P], F32, tag="bank5")
        for t in range(PACK):
            nc.tensor.transpose(factor_rows[:, t, :], factor_cols[:, t : t + 1].to_broadcast([P, P]), ident[:])

        w_bf = sb.tile([P, PAIRS, P, 2], BF16)
        turned_w = ps.tile([P, 1, PAIRS, P], F32, tag="bank0")
        for u in range(PAIRS):
            nc.vector.scalar_tensor_tensor(
                out=w_bf[:, u],
                in0=part[:].rearrange("q (p t) -> q p t", t=PACK)[:, :, 2 * u : 2 * u + 2],
                scalar=part_inv[:],
                in1=factor_rows[:, 2 * u : 2 * u + 2, :].rearrange("q t p -> q p t"),
                op0=ALU.mult,
                op1=ALU.mult,
            )
            nc.tensor.transpose(
                turned_w[:, 0, u, :], w_bf[:, u].rearrange("q p h -> q (p h)").bitcast(F32), ident[:]
            )

        picked3 = sb.tile([P, I], BF16)
        gather_on_scalar(picked3, values3, list1, 0, SCALAR_SLOTS)
        gather_on_vector(picked3, values3, list1, SCALAR_SLOTS, I)
        turned3 = ps.tile([P, 1, PAIRS, P], F32, tag="bank5")
        turn_picked(picked3, turned3[:, 0])

        grouped = sb.tile([P, (BLOCKS + 1) * GROUPED], BF16, tag="values3", align_bytes=64)
        w_grouped = grouped[:, BLOCKS * GROUPED :]
        interleave(nc.vector.tensor_copy, w_grouped, turned_w[:])
        v_codes = sb.tile([P, E], U32, align_bytes=64)
        v_scales = sb.tile([P, E], U8, align_bytes=64)
        w_codes = sb.tile([P, Q], U32, align_bytes=64)
        w_scales = sb.tile([P, Q], U8, align_bytes=64)
        nc.vector.quantize_mx(out=w_codes[:].bitcast(FP8X4), scales=w_scales[:], in_=w_grouped)
        for first_block, end_block, turned_values in ((0, 2, turned01), (2, 3, turned2), (3, 4, turned3)):
            v_grouped = grouped[:, first_block * GROUPED : end_block * GROUPED]
            interleave(nc.scalar.copy, v_grouped, turned_values[:])
            features = slice(first_block * P, end_block * P)
            nc.vector.quantize_mx(out=v_codes[:, features].bitcast(FP8X4), scales=v_scales[:, features], in_=v_grouped)

        change = sb.tile([P, E], F32)
        squares = sb.tile([P, E], F32)
        feature_halves = (slice(0, E // 2), slice(E // 2, E))
        mean_parts = []
        for features, bank in zip(feature_halves, ("bank3", "bank4")):
            o_ps = ps.tile([P, E // 2], F32, tag=bank, name="o_ps")
            nc.tensor.matmul_mx(
                out=o_ps[:],
                lhsT=w_codes[:].bitcast(FP8X4),
                lhsT_scale=w_scales[:],
                rhs=v_codes[:, features].bitcast(FP8X4),
                rhs_scale=v_scales[:, features],
                start=True,
                stop=True,
            )
            nc.vector.tensor_tensor(out=change[:, features], in0=o_ps[:], in1=before_sb[:, features], op=ALU.subtract)
            mean_part = sb.tile([P, 1], F32, name="mean_part_" + bank)
            nc.vector.scalar_tensor_tensor(
                out=squares[:, features],
                in0=change[:, features],
                scalar=1.0 / E,
                in1=change[:, features],
                op0=ALU.mult,
                op1=ALU.mult,
                accum_out=mean_part[:],
            )
            mean_parts.append(mean_part)

        gate_bias = sb.tile([P, 1], F32)
        nc.vector.tensor_scalar(
            out=gate_bias[:], in0=mean_parts[0][:], scalar1=eager_sb[:], scalar2=-1.0, op0=ALU.mult, op1=ALU.add
        )
        gate = sb.tile([P, 1], F32)
        nc.scalar.activation(out=gate[:], in_=mean_parts[1][:], func=ACT.Sigmoid, bias=gate_bias[:], scale=eager_sb[:])

        result = sb.tile([P, E], F32)
        for features, queue in zip(feature_halves, (nc.sync, nc.scalar)):
            nc.vector.scalar_tensor_tensor(
                out=result[:, features],
                in0=change[:, features],
                scalar=gate[:],
                in1=before_sb[:, features],
                op0=ALU.mult,
                op1=ALU.add,
            )
            queue.dma_start(out=out[:, features], in_=result[:, features])
